import numpy as np
import ml_dtypes


def mxq(x, axis, fmt="e4m3"):
    dtype, down = {"e4m3": (ml_dtypes.float8_e4m3fn, 7), "e5m2": (ml_dtypes.float8_e5m2, 14)}[fmt]
    v = np.moveaxis(np.asarray(x, np.float32).astype(ml_dtypes.bfloat16).astype(np.float64), axis, -1)
    blocks = v.reshape(v.shape[:-1] + (-1, 32))
    amax = np.abs(blocks).max(-1, keepdims=True)
    byte = np.maximum(np.where(amax > 0, np.frexp(amax)[1] - 1 + 127, 0) - down, 1)
    scale = np.exp2(byte - 127.0)
    codes = (blocks / scale).astype(np.float32).astype(dtype).astype(np.float64)
    return np.moveaxis((codes * scale).reshape(v.shape), -1, axis)


WIDE = False


def mx_kscale(k, group=512):
    if not WIDE:
        return np.ones(k)
    levels = np.array([10, -10, 5, -5, 0])
    if group != 512:
        return np.exp2(np.random.permutation(np.resize(levels, k // group))).repeat(group)
    if k % 512:
        return np.exp2(np.random.permutation(np.resize(levels, k // 32))).repeat(32)
    a = np.empty((k // 512, 16))
    for p in range(k // 512):
        a[p, :8] = np.random.permutation(np.resize(levels, 8))
        for g in range(8):
            far = levels[np.abs(levels - a[p, g]) >= 10]
            a[p, g + 8] = far[np.random.randint(len(far))]
    return np.exp2(a.ravel()).repeat(32)


def f64(x):
    return np.asarray(x).astype(np.float64)


def striped(idx):
    return np.tile(np.asarray(idx).reshape(-1, 16).T, (8, 1)).astype(np.uint16)


def unstriped(offs):
    return offs[:16].T.reshape(-1).astype(np.int64)


H, KV, D, NQ, N = 4, 1, 256, 512, 512


def setup_inputs():
    n = np.random.standard_normal
    s = mx_kscale(D, 0)[:, None]
    u = mx_kscale(N)
    t = np.random.uniform(0.5, 2.0, N) * u
    v = n((KV, N, 128))
    return {
        "qT": (n((H, D, NQ)) * s * (0.70 / np.sqrt(D))).astype(np.float32),
        "kT": (n((KV, D, N)) / s).astype(np.float32),
        "t": t.reshape(N, 1).astype(np.float32),
        "v": (v / t[:, None]).astype(np.float32),
        "kb": (0.5 * n((N, 1))).astype(np.float32),
        "gn": np.tile(np.random.uniform(0.5, 2.0, 128), (128, 1)).astype(np.float32),
        "og": n((H, NQ, 128)).astype(np.float32),
    }


def reference(qT, kT, t, v, kb, gn, og):
    a = np.repeat(mxq(f64(kT), 1, "e4m3"), H // KV, 0).transpose(0, 2, 1) @ mxq(f64(qT), 1, "e4m3")
    a = a + f64(kb)
    p = np.tanh(a)
    w = p * f64(t)
    y = mxq(w, 1, "e4m3").transpose(0, 2, 1) @ np.repeat(mxq(f64(v), 1, "e4m3"), H // KV, 0)
    y = y / 16.0
    y = y / np.sqrt(np.mean(np.square(y), -1, keepdims=True) + 1e-5) * f64(gn)[:1]
    y = y / (1.0 + np.exp(-f64(og)))
    return y

@@ -1,0 +1,236 @@
+from contextlib import ExitStack
+
+import concourse.mybir as mybir
+
+H, D, NQ, NT, E = 4, 256, 512, 512, 128
+FLOPS = 2 * H * NQ * NT * (D + E)
+
+F32 = mybir.dt.float32
+BF16 = mybir.dt.bfloat16
+U32 = mybir.dt.uint32
+U8 = mybir.dt.uint8
+FP8X4 = mybir.dt.float8_e4m3fn_x4
+ACT = mybir.ActivationFunctionType
+ALU = mybir.AluOpType
+
+P = 128
+ROWS = 64
+PACK = 4
+N = 128
+UNIT = 256
+K_SPLIT = 88
+Q_SPLIT = 176
+
+
+def tile_rows_a_tanh_kb_onorm_gate_kernel(tc, qT, kT, t, v, kb, gn, og, out):
+    nc = tc.nc
+    with ExitStack() as ctx:
+        sb = ctx.enter_context(tc.tile_pool(name="sb", bufs=1))
+        ps = ctx.enter_context(tc.psum_pool(name="ps", bufs=1))
+        ctx.enter_context(tc.manual_schedule())
+
+        def quantise(name, values, words):
+            codes = sb.tile([P, words], U32, name=name + "_codes", align_bytes=64)
+            scales = sb.tile([P, words], U8, name=name + "_scales", align_bytes=64)
+            nc.vector.quantize_mx(out=codes[:].bitcast(FP8X4), scales=scales[:], in_=values)
+            return codes, scales
+
+        k_raw = sb.tile([P, PACK, NT], F32, name="k_raw")
+        k_rows = kT[0].rearrange("(p j) n -> p j n", j=PACK)
+        nc.sync.dma_start(out=k_raw[0:ROWS], in_=k_rows)
+        nc.scalar.dma_start(out=k_raw[ROWS:P], in_=k_rows)
+        kb_sb = sb.tile([P, PACK], F32, name="kb_sb")
+        nc.scalar.dma_start(out=kb_sb[:], in_=kb.rearrange("(s r) o -> s (r o)", r=PACK))
+        t_sb = sb.tile([P, PACK], F32, name="t_sb")
+        nc.scalar.dma_start(out=t_sb[:], in_=t.rearrange("(s r) o -> s (r o)", r=PACK))
+
+        def load_q(name, pair, first, width):
+            raw = sb.tile([P, PACK, width], F32, name=name)
+            rows = qT[2 * pair : 2 * pair + 2].rearrange("h (p j) n -> (h p) j n", j=PACK)
+            nc.sync.dma_start(out=raw[:], in_=rows[:, :, first : first + width])
+            return raw
+
+        qa_raw = load_q("qa_raw", 0, 0, UNIT)
+        qb_raw = load_q("qb_raw", 0, UNIT, UNIT)
+        v_raw = sb.tile([P, PACK, E], F32, name="v_raw")
+        nc.sync.dma_start(out=v_raw[:], in_=v[0].rearrange("(s r) e -> s r e", r=PACK))
+        qc_raw = load_q("qc_raw", 1, 0, NQ)
+        gn_sb = sb.tile([P, E], F32, name="gn_sb")
+        nc.sync.dma_start(out=gn_sb[:], in_=gn)
+        og_sb = sb.tile([P, 2 * H, 2 * E], F32, name="og_sb")
+        nc.sync.dma_start(out=og_sb[:], in_=og.rearrange("h (a m c) e -> m (h a) (c e)", a=2, c=2))
+
+        k_bf = sb.tile([P, PACK, N, PACK], BF16, name="k_bf", align_bytes=64)
+
+        def deal_keys(copy, s0, s1):
+            copy(
+                out=k_bf[:, :, s0:s1, :].rearrange("p r s j -> p s j r"),
+                in_=k_raw[:, :, PACK * s0 : PACK * s1].rearrange("p j (s r) -> p s j r", r=PACK),
+            )
+
+        def interleave(copy, packed, raw, c0, c1):
+            copy(
+                out=packed[:, c0:c1, :].rearrange("p (c i) j -> p c j i", i=2),
+                in_=raw[:, :, c0:c1].rearrange("p j (c i) -> p c j i", i=2),
+            )
+
+        deal_keys(nc.vector.tensor_copy, 0, K_SPLIT)
+        deal_keys(nc.scalar.copy, K_SPLIT, N)
+        k_codes, k_scales = quantise("k", k_bf[:].rearrange("p r s j -> p (r s j)"), NT)
+
+        qa_bf = sb.tile([P, UNIT, PACK], BF16, name="qa_bf", align_bytes=64)
+        interleave(nc.vector.tensor_copy, qa_bf, qa_raw, 0, Q_SPLIT)
+        interleave(nc.scalar.copy, qa_bf, qa_raw, Q_SPLIT, UNIT)
+        qa = quantise("qa", qa_bf[:].rearrange("p n j -> p (n j)"), UNIT)
+
+        qb_bf = sb.tile([P, UNIT, PACK], BF16, name="qb_bf", align_bytes=64)
+        interleave(nc.vector.tensor_copy, qb_bf, qb_raw, 0, UNIT)
+        v_bf = sb.tile([P, E, PACK], BF16, name="v_bf", align_bytes=64)
+        interleave(nc.vector.tensor_copy, v_bf, v_raw, 0, E)
+        qb = quantise("qb", qb_bf[:].rearrange("p n j -> p (n j)"), UNIT)
+        v_codes, v_scales = quantise("v", v_bf[:].rearrange("p n j -> p (n j)"), E)
+
+        units = [(2 * pair + g, a) for pair in range(2) for a in range(2) for g in range(2)]
+        banks = [[ps.tile([P, 2, UNIT], F32, name="scores_%d_%d" % (g, b)) for b in range(2)] for g in range(2)]
+        y = [ps.tile([P, 4, E], F32, name="y_%d" % h) for h in range(H)]
+        q_ops = {(0, 0): (qa, 0), (0, 1): (qb, 0)}
+        t_rep = t_sb[:].unsqueeze(1).unsqueeze(3).to_broadcast([P, UNIT // 2, PACK, 2])
+
+        def scores_and_tanh(u):
+            h, a = units[u]
+            g = h % 2
+            rows = slice(ROWS * g, ROWS * (g + 1))
+            (q_codes, q_scales), first = q_ops[(h // 2, a)]
+            p = sb.tile([P, PACK, UNIT], F32, name="p_%d" % u)
+            for b in range(2):
+                for rr in range(2):
+                    keys = slice(N * (2 * b + rr), N * (2 * b + rr + 1))
+                    for c in range(2):
+                        cols = slice(first + N * c, first + N * (c + 1))
+                        nc.tensor.matmul_mx(
+                            out=banks[g][b][:, rr, N * c : N * (c + 1)],
+                            lhsT=k_codes[rows, keys].bitcast(FP8X4),
+                            lhsT_scale=k_scales[rows, keys],
+                            rhs=q_codes[rows, cols].bitcast(FP8X4),
+                            rhs_scale=q_scales[rows, cols],
+                            start=True,
+                            stop=True,
+                        )
+                for rr in range(2):
+                    r = 2 * b + rr
+                    nc.scalar.activation(
+                        out=p[:, r, :].rearrange("p (c m) -> p c m", c=2),
+                        in_=banks[g][b][:, rr, :].rearrange("p (m c) -> p c m", c=2),
+                        func=ACT.Tanh,
+                        bias=kb_sb[:, r : r + 1],
+                    )
+            return p
+
+        def weigh(u, p):
+            w = sb.tile([P, UNIT, PACK], BF16, name="w_%d" % u, align_bytes=64)
+            nc.vector.tensor_tensor(
+                out=w[:].rearrange("p (c i) r -> p c r i", i=2),
+                in0=p[:].rearrange("p r (c i) -> p c r i", i=2),
+                in1=t_rep,
+                op=ALU.mult,
+            )
+            return w
+
+        def quantise_w(u, w):
+            return quantise("w_%d" % u, w[:].rearrange("p n r -> p (n r)"), UNIT)
+
+        def values(u, wq):
+            h, a = units[u]
+            for c in range(2):
+                cols = slice(N * c, N * (c + 1))
+                nc.tensor.matmul_mx(
+                    out=y[h][:, 2 * a + c, :],
+                    lhsT=wq[0][:, cols].bitcast(FP8X4),
+                    lhsT_scale=wq[1][:, cols],
+                    rhs=v_codes[:].bitcast(FP8X4),
+                    rhs_scale=v_scales[:],
+                    start=True,
+                    stop=True,
+                )
+
+        p_tiles = [scores_and_tanh(u) for u in range(4)]
+        w_tiles = [weigh(0, p_tiles[0])]
+        qc_bf = sb.tile([P, NQ, PACK], BF16, name="qc_bf", align_bytes=64)
+        interleave(nc.vector.tensor_copy, qc_bf, qc_raw, 0, NQ)
+        w_q = [quantise_w(0, w_tiles[0])]
+        qc = quantise("qc", qc_bf[:].rearrange("p n j -> p (n j)"), NQ)
+        q_ops[(1, 0)] = (qc, 0)
+        q_ops[(1, 1)] = (qc, UNIT)
+        p_tiles.extend(scores_and_tanh(u) for u in range(4, 8))
+
+        w_tiles.append(weigh(1, p_tiles[1]))
+        for u in range(2, 8):
+            w_tiles.append(weigh(u, p_tiles[u]))
+            w_q.append(quantise_w(u - 1, w_tiles[u - 1]))
+        for u in range(7):
+            values(u, w_q[u])
+
+        sumsq = sb.tile([P, 4 * H], F32, name="sumsq")
+        rs = sb.tile([P, 4 * H], F32, name="rs")
+        squares = sb.tile([P, 4 * H, E], BF16, name="squares")
+        th = [sb.tile([P, 4, E], F32, name="th_%d" % h) for h in range(H)]
+        gate = [sb.tile([P, 4, E], F32, name="gate_%d" % h) for h in range(H)]
+        res = [sb.tile([P, 4, E], F32, name="res_%d" % h) for h in range(H)]
+        gn_rep = gn_sb[:].unsqueeze(1).to_broadcast([P, 4, E])
+
+        def sum_squares(h):
+            for c in range(4):
+                nc.scalar.activation(
+                    out=squares[:, 4 * h + c, :],
+                    in_=y[h][:, c, :],
+                    func=ACT.Square,
+                    accum_out=sumsq[:, 4 * h + c : 4 * h + c + 1],
+                )
+
+        def inverse_root(h):
+            nc.scalar.activation(
+                out=rs[:, 4 * h : 4 * h + 4],
+                in_=sumsq[:, 4 * h : 4 * h + 4],
+                func=ACT.Abs_reciprocal_sqrt,
+                scale=1.0 / 32.0,
+                bias=1024.0 * 1e-5,
+            )
+
+        def make_gate(h):
+            nc.vector.scalar_tensor_tensor(
+                out=gate[h][:], in0=th[h][:], scalar=1.0, in1=gn_rep, op0=ALU.add, op1=ALU.mult
+            )
+
+        def finish(h, halves):
+            dst = out[h].rearrange("(a m c) e -> m a (c e)", a=2, c=2)
+            src = res[h][:].rearrange("p (a c) e -> p a (c e)", a=2)
+            for part in halves:
+                for c in range(2 * part.start, 2 * part.stop):
+                    nc.vector.scalar_tensor_tensor(
+                        out=res[h][:, c, :],
+                        in0=y[h][:, c, :],
+                        scalar=rs[:, 4 * h + c : 4 * h + c + 1],
+                        in1=gate[h][:, c, :],
+                        op0=ALU.mult,
+                        op1=ALU.mult,
+                    )
+                nc.sync.dma_start(out=dst[:, part, :], in_=src[:, part, :])
+
+        sum_squares(0)
+        for h in range(H):
+            nc.scalar.activation(
+                out=th[h][:].rearrange("p (a c) e -> p a (c e)", a=2),
+                in_=og_sb[:, 2 * h : 2 * h + 2, :],
+                func=ACT.Tanh,
+                scale=0.5,
+            )
+        inverse_root(0)
+        make_gate(0)
+        values(7, quantise_w(7, w_tiles[7]))
+        for h in range(1, H):
+            sum_squares(h)
+            inverse_root(h)
+        for h in range(1, H):
+            make_gate(h)
+            finish(h - 1, [slice(0, 2)])
+        finish(H - 1, [slice(0, 1), slice(1, 2)])

@@ -18,8 +18,6 @@ ROWS = 64
 PACK = 4
 N = 128
 UNIT = 256
-K_SPLIT = 88
-Q_SPLIT = 176
 
 
 def tile_rows_a_tanh_kb_onorm_gate_kernel(tc, qT, kT, t, v, kb, gn, og, out):
@@ -39,10 +37,6 @@ def tile_rows_a_tanh_kb_onorm_gate_kernel(tc, qT, kT, t, v, kb, gn, og, out):
         k_rows = kT[0].rearrange("(p j) n -> p j n", j=PACK)
         nc.sync.dma_start(out=k_raw[0:ROWS], in_=k_rows)
         nc.scalar.dma_start(out=k_raw[ROWS:P], in_=k_rows)
-        kb_sb = sb.tile([P, PACK], F32, name="kb_sb")
-        nc.scalar.dma_start(out=kb_sb[:], in_=kb.rearrange("(s r) o -> s (r o)", r=PACK))
-        t_sb = sb.tile([P, PACK], F32, name="t_sb")
-        nc.scalar.dma_start(out=t_sb[:], in_=t.rearrange("(s r) o -> s (r o)", r=PACK))
 
         def load_q(name, pair, first, width):
             raw = sb.tile([P, PACK, width], F32, name=name)
@@ -51,6 +45,10 @@ def tile_rows_a_tanh_kb_onorm_gate_kernel(tc, qT, kT, t, v, kb, gn, og, out):
             return raw
 
         qa_raw = load_q("qa_raw", 0, 0, UNIT)
+        kb_sb = sb.tile([P, PACK], F32, name="kb_sb")
+        nc.sync.dma_start(out=kb_sb[:], in_=kb.rearrange("(s r) o -> s (r o)", r=PACK))
+        t_sb = sb.tile([P, PACK], F32, name="t_sb")
+        nc.sync.dma_start(out=t_sb[:], in_=t.rearrange("(s r) o -> s (r o)", r=PACK))
         qb_raw = load_q("qb_raw", 0, UNIT, UNIT)
         v_raw = sb.tile([P, PACK, E], F32, name="v_raw")
         nc.sync.dma_start(out=v_raw[:], in_=v[0].rearrange("(s r) e -> s r e", r=PACK))
@@ -60,71 +58,97 @@ def tile_rows_a_tanh_kb_onorm_gate_kernel(tc, qT, kT, t, v, kb, gn, og, out):
         og_sb = sb.tile([P, 2 * H, 2 * E], F32, name="og_sb")
         nc.sync.dma_start(out=og_sb[:], in_=og.rearrange("h (a m c) e -> m (h a) (c e)", a=2, c=2))
 
-        k_bf = sb.tile([P, PACK, N, PACK], BF16, name="k_bf", align_bytes=64)
-
-        def deal_keys(copy, s0, s1):
+        def deal_keys(copy, b):
+            dealt = sb.tile([P, 2, N, PACK], BF16, name="k_bf_%d" % b, align_bytes=64)
             copy(
-                out=k_bf[:, :, s0:s1, :].rearrange("p r s j -> p s j r"),
-                in_=k_raw[:, :, PACK * s0 : PACK * s1].rearrange("p j (s r) -> p s j r", r=PACK),
+                out=dealt[:].rearrange("p r s j -> p s j r"),
+                in_=k_raw[:].rearrange("p j (s r) -> p s j r", r=PACK)[:, :, :, 2 * b : 2 * b + 2],
             )
+            return dealt[:].rearrange("p r s j -> p (r s j)")
 
-        def interleave(copy, packed, raw, c0, c1):
+        def interleave(copy, name, raw, c0, c1):
+            packed = sb.tile([P, c1 - c0, PACK], BF16, name=name, align_bytes=64)
             copy(
-                out=packed[:, c0:c1, :].rearrange("p (c i) j -> p c j i", i=2),
+                out=packed[:].rearrange("p (c i) j -> p c j i", i=2),
                 in_=raw[:, :, c0:c1].rearrange("p j (c i) -> p c j i", i=2),
             )
+            return packed[:].rearrange("p n j -> p (n j)")
 
-        deal_keys(nc.vector.tensor_copy, 0, K_SPLIT)
-        deal_keys(nc.scalar.copy, K_SPLIT, N)
-        k_codes, k_scales = quantise("k", k_bf[:].rearrange("p r s j -> p (r s j)"), NT)
+        k_lo = deal_keys(nc.vector.tensor_copy, 0)
+        k_hi = deal_keys(nc.scalar.copy, 1)
+        k_ops = [quantise("k_lo", k_lo, 2 * N), quantise("k_hi", k_hi, 2 * N)]
 
-        qa_bf = sb.tile([P, UNIT, PACK], BF16, name="qa_bf", align_bytes=64)
-        interleave(nc.vector.tensor_copy, qa_bf, qa_raw, 0, Q_SPLIT)
-        interleave(nc.scalar.copy, qa_bf, qa_raw, Q_SPLIT, UNIT)
-        qa = quantise("qa", qa_bf[:].rearrange("p n j -> p (n j)"), UNIT)
+        qa_lo = interleave(nc.vector.tensor_copy, "qa_lo", qa_raw, 0, N)
+        qa_hi = interleave(nc.scalar.copy, "qa_hi", qa_raw, N, UNIT)
+        q_ops = {(0, 0, 0): (quantise("qa_lo", qa_lo, N), 0), (0, 0, 1): (quantise("qa_hi", qa_hi, N), 0)}
 
-        qb_bf = sb.tile([P, UNIT, PACK], BF16, name="qb_bf", align_bytes=64)
-        interleave(nc.vector.tensor_copy, qb_bf, qb_raw, 0, UNIT)
-        v_bf = sb.tile([P, E, PACK], BF16, name="v_bf", align_bytes=64)
-        interleave(nc.vector.tensor_copy, v_bf, v_raw, 0, E)
-        qb = quantise("qb", qb_bf[:].rearrange("p n j -> p (n j)"), UNIT)
-        v_codes, v_scales = quantise("v", v_bf[:].rearrange("p n j -> p (n j)"), E)
+        t_pairs = sb.tile([P, PACK, 2], F32, name="t_pairs")
+        nc.vector.tensor_copy(out=t_pairs[:], in_=t_sb[:].unsqueeze(2).to_broadcast([P, PACK, 2]))
+        qb_bf = interleave(nc.vector.tensor_copy, "qb_bf", qb_raw, 0, UNIT)
+        v_bf = interleave(nc.vector.tensor_copy, "v_bf", v_raw, 0, E)
+        qb = quantise("qb", qb_bf, UNIT)
+        v_codes, v_scales = quantise("v", v_bf, E)
+        for c in range(2):
+            q_ops[(0, 1, c)] = (qb, N * c)
 
         units = [(2 * pair + g, a) for pair in range(2) for a in range(2) for g in range(2)]
         banks = [[ps.tile([P, 2, UNIT], F32, name="scores_%d_%d" % (g, b)) for b in range(2)] for g in range(2)]
         y = [ps.tile([P, 4, E], F32, name="y_%d" % h) for h in range(H)]
-        q_ops = {(0, 0): (qa, 0), (0, 1): (qb, 0)}
-        t_rep = t_sb[:].unsqueeze(1).unsqueeze(3).to_broadcast([P, UNIT // 2, PACK, 2])
+        t_rep = t_pairs[:].unsqueeze(1).to_broadcast([P, UNIT // 2, PACK, 2])
 
-        def scores_and_tanh(u):
+        p_tiles = [sb.tile([P, PACK, UNIT], F32, name="p_%d" % u) for u in range(8)]
+
+        def score_calls(f):
+            u, b = divmod(f, 2)
             h, a = units[u]
             g = h % 2
             rows = slice(ROWS * g, ROWS * (g + 1))
-            (q_codes, q_scales), first = q_ops[(h // 2, a)]
-            p = sb.tile([P, PACK, UNIT], F32, name="p_%d" % u)
-            for b in range(2):
-                for rr in range(2):
-                    keys = slice(N * (2 * b + rr), N * (2 * b + rr + 1))
-                    for c in range(2):
-                        cols = slice(first + N * c, first + N * (c + 1))
-                        nc.tensor.matmul_mx(
+            k_codes, k_scales = k_ops[b]
+            calls = []
+            for rr in range(2):
+                keys = slice(N * rr, N * (rr + 1))
+                for c in range(2):
+                    (q_codes, q_scales), first = q_ops[(h // 2, a, c)]
+                    cols = slice(first, first + N)
+                    calls.append(
+                        dict(
                             out=banks[g][b][:, rr, N * c : N * (c + 1)],
                             lhsT=k_codes[rows, keys].bitcast(FP8X4),
                             lhsT_scale=k_scales[rows, keys],
                             rhs=q_codes[rows, cols].bitcast(FP8X4),
                             rhs_scale=q_scales[rows, cols],
-                            start=True,
-                            stop=True,
                         )
-                for rr in range(2):
-                    r = 2 * b + rr
-                    nc.scalar.activation(
-                        out=p[:, r, :].rearrange("p (c m) -> p c m", c=2),
-                        in_=banks[g][b][:, rr, :].rearrange("p (m c) -> p c m", c=2),
-                        func=ACT.Tanh,
-                        bias=kb_sb[:, r : r + 1],
                     )
-            return p
+            return calls
+
+        def fill(*fs):
+            for calls in zip(*[score_calls(f) for f in fs]):
+                for call in calls:
+                    nc.tensor.matmul_mx(start=True, stop=True, **call)
+
+        def tanh(f):
+            u, b = divmod(f, 2)
+            g = units[u][0] % 2
+            for rr in range(2):
+                r = 2 * b + rr
+                nc.scalar.activation(
+                    out=p_tiles[u][:, r, :].rearrange("p (c m) -> p c m", c=2),
+                    in_=banks[g][b][:, rr, :].rearrange("p (m c) -> p c m", c=2),
+                    func=ACT.Tanh,
+                    bias=kb_sb[:, r : r + 1],
+                )
+
+        def scores_and_tanh(f0):
+            fill(f0)
+            fill(f0 + 1, f0 + 2)
+            tanh(f0)
+            for f in (f0 + 3, f0 + 5):
+                fill(f, f + 1)
+                tanh(f - 2)
+                tanh(f - 1)
+            fill(f0 + 7)
+            for f in range(f0 + 5, f0 + 8):
+                tanh(f)
 
         def weigh(u, p):
             w = sb.tile([P, UNIT, PACK], BF16, name="w_%d" % u, align_bytes=64)
@@ -153,15 +177,15 @@ def tile_rows_a_tanh_kb_onorm_gate_kernel(tc, qT, kT, t, v, kb, gn, og, out):
                     stop=True,
                 )
 
-        p_tiles = [scores_and_tanh(u) for u in range(4)]
+        scores_and_tanh(0)
         w_tiles = [weigh(0, p_tiles[0])]
-        qc_bf = sb.tile([P, NQ, PACK], BF16, name="qc_bf", align_bytes=64)
-        interleave(nc.vector.tensor_copy, qc_bf, qc_raw, 0, NQ)
+        qc_bf = interleave(nc.vector.tensor_copy, "qc_bf", qc_raw, 0, NQ)
         w_q = [quantise_w(0, w_tiles[0])]
-        qc = quantise("qc", qc_bf[:].rearrange("p n j -> p (n j)"), NQ)
-        q_ops[(1, 0)] = (qc, 0)
-        q_ops[(1, 1)] = (qc, UNIT)
-        p_tiles.extend(scores_and_tanh(u) for u in range(4, 8))
+        qc = quantise("qc", qc_bf, NQ)
+        for a in range(2):
+            for c in range(2):
+                q_ops[(1, a, c)] = (qc, UNIT * a + N * c)
+        scores_and_tanh(8)
 
         w_tiles.append(weigh(1, p_tiles[1]))
         for u in range(2, 8):

from contextlib import ExitStack

import concourse.mybir as mybir

H, D, NQ, NT, E = 4, 256, 512, 512, 128
FLOPS = 2 * H * NQ * NT * (D + E)

F32 = mybir.dt.float32
BF16 = mybir.dt.bfloat16
U32 = mybir.dt.uint32
U8 = mybir.dt.uint8
FP8X4 = mybir.dt.float8_e4m3fn_x4
ACT = mybir.ActivationFunctionType
ALU = mybir.AluOpType

P = 128
ROWS = 64
PACK = 4
N = 128
UNIT = 256


def tile_rows_a_tanh_kb_onorm_gate_kernel(tc, qT, kT, t, v, kb, gn, og, out):
    nc = tc.nc
    with ExitStack() as ctx:
        sb = ctx.enter_context(tc.tile_pool(name="sb", bufs=1))
        ps = ctx.enter_context(tc.psum_pool(name="ps", bufs=1))
        ctx.enter_context(tc.manual_schedule())

        def quantise(name, values, words):
            codes = sb.tile([P, words], U32, name=name + "_codes", align_bytes=64)
            scales = sb.tile([P, words], U8, name=name + "_scales", align_bytes=64)
            nc.vector.quantize_mx(out=codes[:].bitcast(FP8X4), scales=scales[:], in_=values)
            return codes, scales

        k_raw = sb.tile([P, PACK, NT], F32, name="k_raw")
        k_rows = kT[0].rearrange("(p j) n -> p j n", j=PACK)
        nc.sync.dma_start(out=k_raw[0:ROWS], in_=k_rows)
        nc.scalar.dma_start(out=k_raw[ROWS:P], in_=k_rows)

        def load_q(name, pair, first, width):
            raw = sb.tile([P, PACK, width], F32, name=name)
            rows = qT[2 * pair : 2 * pair + 2].rearrange("h (p j) n -> (h p) j n", j=PACK)
            nc.sync.dma_start(out=raw[:], in_=rows[:, :, first : first + width])
            return raw

        qa_raw = load_q("qa_raw", 0, 0, UNIT)
        kb_sb = sb.tile([P, PACK], F32, name="kb_sb")
        nc.sync.dma_start(out=kb_sb[:], in_=kb.rearrange("(s r) o -> s (r o)", r=PACK))
        t_sb = sb.tile([P, PACK], F32, name="t_sb")
        nc.sync.dma_start(out=t_sb[:], in_=t.rearrange("(s r) o -> s (r o)", r=PACK))
        qb_raw = load_q("qb_raw", 0, UNIT, UNIT)
        v_raw = sb.tile([P, PACK, E], F32, name="v_raw")
        nc.sync.dma_start(out=v_raw[:], in_=v[0].rearrange("(s r) e -> s r e", r=PACK))
        qc_raw = load_q("qc_raw", 1, 0, NQ)
        gn_sb = sb.tile([P, E], F32, name="gn_sb")
        nc.sync.dma_start(out=gn_sb[:], in_=gn)
        og_sb = sb.tile([P, 2 * H, 2 * E], F32, name="og_sb")
        nc.sync.dma_start(out=og_sb[:], in_=og.rearrange("h (a m c) e -> m (h a) (c e)", a=2, c=2))

        def deal_keys(copy, b):
            dealt = sb.tile([P, 2, N, PACK], BF16, name="k_bf_%d" % b, align_bytes=64)
            copy(
                out=dealt[:].rearrange("p r s j -> p s j r"),
                in_=k_raw[:].rearrange("p j (s r) -> p s j r", r=PACK)[:, :, :, 2 * b : 2 * b + 2],
            )
            return dealt[:].rearrange("p r s j -> p (r s j)")

        def interleave(copy, name, raw, c0, c1):
            packed = sb.tile([P, c1 - c0, PACK], BF16, name=name, align_bytes=64)
            copy(
                out=packed[:].rearrange("p (c i) j -> p c j i", i=2),
                in_=raw[:, :, c0:c1].rearrange("p j (c i) -> p c j i", i=2),
            )
            return packed[:].rearrange("p n j -> p (n j)")

        k_lo = deal_keys(nc.vector.tensor_copy, 0)
        k_hi = deal_keys(nc.scalar.copy, 1)
        k_ops = [quantise("k_lo", k_lo, 2 * N), quantise("k_hi", k_hi, 2 * N)]

        qa_lo = interleave(nc.vector.tensor_copy, "qa_lo", qa_raw, 0, N)
        qa_hi = interleave(nc.scalar.copy, "qa_hi", qa_raw, N, UNIT)
        q_ops = {(0, 0, 0): (quantise("qa_lo", qa_lo, N), 0), (0, 0, 1): (quantise("qa_hi", qa_hi, N), 0)}

        t_pairs = sb.tile([P, PACK, 2], F32, name="t_pairs")
        nc.vector.tensor_copy(out=t_pairs[:], in_=t_sb[:].unsqueeze(2).to_broadcast([P, PACK, 2]))
        qb_bf = interleave(nc.vector.tensor_copy, "qb_bf", qb_raw, 0, UNIT)
        v_bf = interleave(nc.vector.tensor_copy, "v_bf", v_raw, 0, E)
        qb = quantise("qb", qb_bf, UNIT)
        v_codes, v_scales = quantise("v", v_bf, E)
        for c in range(2):
            q_ops[(0, 1, c)] = (qb, N * c)

        units = [(2 * pair + g, a) for pair in range(2) for a in range(2) for g in range(2)]
        banks = [[ps.tile([P, 2, UNIT], F32, name="scores_%d_%d" % (g, b)) for b in range(2)] for g in range(2)]
        y = [ps.tile([P, 4, E], F32, name="y_%d" % h) for h in range(H)]
        t_rep = t_pairs[:].unsqueeze(1).to_broadcast([P, UNIT // 2, PACK, 2])

        p_tiles = [sb.tile([P, PACK, UNIT], F32, name="p_%d" % u) for u in range(8)]

        def score_calls(f):
            u, b = divmod(f, 2)
            h, a = units[u]
            g = h % 2
            rows = slice(ROWS * g, ROWS * (g + 1))
            k_codes, k_scales = k_ops[b]
            calls = []
            for rr in range(2):
                keys = slice(N * rr, N * (rr + 1))
                for c in range(2):
                    (q_codes, q_scales), first = q_ops[(h // 2, a, c)]
                    cols = slice(first, first + N)
                    calls.append(
                        dict(
                            out=banks[g][b][:, rr, N * c : N * (c + 1)],
                            lhsT=k_codes[rows, keys].bitcast(FP8X4),
                            lhsT_scale=k_scales[rows, keys],
                            rhs=q_codes[rows, cols].bitcast(FP8X4),
                            rhs_scale=q_scales[rows, cols],
                        )
                    )
            return calls

        def fill(*fs):
            for calls in zip(*[score_calls(f) for f in fs]):
                for call in calls:
                    nc.tensor.matmul_mx(start=True, stop=True, **call)

        def tanh(f):
            u, b = divmod(f, 2)
            g = units[u][0] % 2
            for rr in range(2):
                r = 2 * b + rr
                nc.scalar.activation(
                    out=p_tiles[u][:, r, :].rearrange("p (c m) -> p c m", c=2),
                    in_=banks[g][b][:, rr, :].rearrange("p (m c) -> p c m", c=2),
                    func=ACT.Tanh,
                    bias=kb_sb[:, r : r + 1],
                )

        def scores_and_tanh(f0):
            fill(f0)
            fill(f0 + 1, f0 + 2)
            tanh(f0)
            for f in (f0 + 3, f0 + 5):
                fill(f, f + 1)
                tanh(f - 2)
                tanh(f - 1)
            fill(f0 + 7)
            for f in range(f0 + 5, f0 + 8):
                tanh(f)

        def weigh(u, p):
            w = sb.tile([P, UNIT, PACK], BF16, name="w_%d" % u, align_bytes=64)
            nc.vector.tensor_tensor(
                out=w[:].rearrange("p (c i) r -> p c r i", i=2),
                in0=p[:].rearrange("p r (c i) -> p c r i", i=2),
                in1=t_rep,
                op=ALU.mult,
            )
            return w

        def quantise_w(u, w):
            return quantise("w_%d" % u, w[:].rearrange("p n r -> p (n r)"), UNIT)

        def values(u, wq):
            h, a = units[u]
            for c in range(2):
                cols = slice(N * c, N * (c + 1))
                nc.tensor.matmul_mx(
                    out=y[h][:, 2 * a + c, :],
                    lhsT=wq[0][:, cols].bitcast(FP8X4),
                    lhsT_scale=wq[1][:, cols],
                    rhs=v_codes[:].bitcast(FP8X4),
                    rhs_scale=v_scales[:],
                    start=True,
                    stop=True,
                )

        scores_and_tanh(0)
        w_tiles = [weigh(0, p_tiles[0])]
        qc_bf = interleave(nc.vector.tensor_copy, "qc_bf", qc_raw, 0, NQ)
        w_q = [quantise_w(0, w_tiles[0])]
        qc = quantise("qc", qc_bf, NQ)
        for a in range(2):
            for c in range(2):
                q_ops[(1, a, c)] = (qc, UNIT * a + N * c)
        scores_and_tanh(8)

        w_tiles.append(weigh(1, p_tiles[1]))
        for u in range(2, 8):
            w_tiles.append(weigh(u, p_tiles[u]))
            w_q.append(quantise_w(u - 1, w_tiles[u - 1]))
        for u in range(7):
            values(u, w_q[u])

        sumsq = sb.tile([P, 4 * H], F32, name="sumsq")
        rs = sb.tile([P, 4 * H], F32, name="rs")
        squares = sb.tile([P, 4 * H, E], BF16, name="squares")
        th = [sb.tile([P, 4, E], F32, name="th_%d" % h) for h in range(H)]
        gate = [sb.tile([P, 4, E], F32, name="gate_%d" % h) for h in range(H)]
        res = [sb.tile([P, 4, E], F32, name="res_%d" % h) for h in range(H)]
        gn_rep = gn_sb[:].unsqueeze(1).to_broadcast([P, 4, E])

        def sum_squares(h):
            for c in range(4):
                nc.scalar.activation(
                    out=squares[:, 4 * h + c, :],
                    in_=y[h][:, c, :],
                    func=ACT.Square,
                    accum_out=sumsq[:, 4 * h + c : 4 * h + c + 1],
                )

        def inverse_root(h):
            nc.scalar.activation(
                out=rs[:, 4 * h : 4 * h + 4],
                in_=sumsq[:, 4 * h : 4 * h + 4],
                func=ACT.Abs_reciprocal_sqrt,
                scale=1.0 / 32.0,
                bias=1024.0 * 1e-5,
            )

        def make_gate(h):
            nc.vector.scalar_tensor_tensor(
                out=gate[h][:], in0=th[h][:], scalar=1.0, in1=gn_rep, op0=ALU.add, op1=ALU.mult
            )

        def finish(h, halves):
            dst = out[h].rearrange("(a m c) e -> m a (c e)", a=2, c=2)
            src = res[h][:].rearrange("p (a c) e -> p a (c e)", a=2)
            for part in halves:
                for c in range(2 * part.start, 2 * part.stop):
                    nc.vector.scalar_tensor_tensor(
                        out=res[h][:, c, :],
                        in0=y[h][:, c, :],
                        scalar=rs[:, 4 * h + c : 4 * h + c + 1],
                        in1=gate[h][:, c, :],
                        op0=ALU.mult,
                        op1=ALU.mult,
                    )
                nc.sync.dma_start(out=dst[:, part, :], in_=src[:, part, :])

        sum_squares(0)
        for h in range(H):
            nc.scalar.activation(
                out=th[h][:].rearrange("p (a c) e -> p a (c e)", a=2),
                in_=og_sb[:, 2 * h : 2 * h + 2, :],
                func=ACT.Tanh,
                scale=0.5,
            )
        inverse_root(0)
        make_gate(0)
        values(7, quantise_w(7, w_tiles[7]))
        for h in range(1, H):
            sum_squares(h)
            inverse_root(h)
        for h in range(1, H):
            make_gate(h)
            finish(h - 1, [slice(0, 2)])
        finish(H - 1, [slice(0, 1), slice(1, 2)])
